import numpy as np
import ml_dtypes


def mxq(x, axis, fmt="e4m3"):
    dtype, down = {"e4m3": (ml_dtypes.float8_e4m3fn, 7), "e5m2": (ml_dtypes.float8_e5m2, 14)}[fmt]
    v = np.moveaxis(np.asarray(x, np.float32).astype(ml_dtypes.bfloat16).astype(np.float64), axis, -1)
    blocks = v.reshape(v.shape[:-1] + (-1, 32))
    amax = np.abs(blocks).max(-1, keepdims=True)
    byte = np.maximum(np.where(amax > 0, np.frexp(amax)[1] - 1 + 127, 0) - down, 1)
    scale = np.exp2(byte - 127.0)
    codes = (blocks / scale).astype(np.float32).astype(dtype).astype(np.float64)
    return np.moveaxis((codes * scale).reshape(v.shape), -1, axis)


WIDE = False


def mx_kscale(k):
    if not WIDE:
        return np.ones(k)
    levels = np.array([10, -10, 5, -5, 0])
    if k % 512:
        return np.exp2(np.random.permutation(np.resize(levels, k // 32))).repeat(32)
    a = np.empty((k // 512, 16))
    for p in range(k // 512):
        a[p, :8] = np.random.permutation(np.resize(levels, 8))
        for g in range(8):
            far = levels[np.abs(levels - a[p, g]) >= 10]
            a[p, g + 8] = far[np.random.randint(len(far))]
    return np.exp2(a.ravel()).repeat(32)


BF16 = ml_dtypes.bfloat16


def bf(x):
    return np.asarray(x, np.float32).astype(BF16)


def f64(x):
    return np.asarray(x).astype(np.float64)


E2M1 = np.array([0.0, 0.5, 1.0, 1.5, 2.0, 3.0, 4.0, 6.0, -0.0, -0.5, -1.0, -1.5, -2.0, -3.0, -4.0, -6.0])


def pack_weight(w, fmt):
    k, n = w.shape
    w = f64(bf(w)).reshape(k // 32, 32, n)
    amax = np.abs(w).max(1)
    if fmt == "e4m3":
        byte = np.frexp(amax)[1] - 1 + 127 - 7
    else:
        mant, ex = np.frexp(amax / 6.0)
        byte = np.where(mant > 0.5, ex, ex - 1) + 127
    byte = np.clip(np.where(amax > 0, byte, 1), 1, 254)
    scaled = (w * np.exp2(127.0 - byte)[:, None, :]).reshape(k, n).astype(np.float32)
    by_word = np.ascontiguousarray(scaled.reshape(k // 512, 128, 4, n).transpose(0, 1, 3, 2))
    if fmt == "e4m3":
        words = by_word.astype(ml_dtypes.float8_e4m3fn).view(np.uint8)
    else:
        c = by_word.astype(ml_dtypes.float4_e2m1fn).view(np.uint8) & 0xF
        words = c[..., 0::2] | (c[..., 1::2] << 4)
    return np.ascontiguousarray(words), np.ascontiguousarray(byte.astype(np.uint8).reshape(k // 512, 16, n))


def unpack_weight(words, scales, fmt):
    g, p, n, _ = words.shape
    if fmt == "e4m3":
        vals = np.ascontiguousarray(words).view(ml_dtypes.float8_e4m3fn).astype(np.float64)
    else:
        nib = np.empty((g, p, n, 4), np.uint8)
        nib[..., 0::2] = words & 0xF
        nib[..., 1::2] = words >> 4
        vals = E2M1[nib]
    vals = vals * np.repeat(np.exp2(scales.astype(np.float64) - 127.0), 8, axis=1)[..., None]
    return vals.transpose(0, 1, 3, 2).reshape(g * 512, n)
def pack4(w):
    words, scales = pack_weight(w, "e2m1")
    return words.reshape(words.shape[0], 128, -1), scales


def unpack4(words, scales):
    return unpack_weight(words.reshape(words.shape[0], 128, -1, 2), scales, "e2m1")


M, K, F, P, N = 1024, 1024, 1024, 3, 1024

BIAS = 0.4


def draw0():
    s, t = mx_kscale(K), mx_kscale(F)
    w = np.random.standard_normal((K, P * F)) / np.sqrt(K) / s[:, None] * np.tile(t, P)
    v = np.random.standard_normal((F, N)) / np.sqrt(F) / t[:, None]
    w_words, w_scales = pack4(w)
    v_words, v_scales = pack_weight(v, "e4m3")
    return {"x": bf(np.random.standard_normal((M, K)) * s),
            "w_words": w_words,
            "w_scales": w_scales,
            "b": bf(BIAS * np.random.standard_normal((P, F)) * t),
            "v_words": v_words,
            "v_scales": v_scales,
            "c": bf(BIAS * np.random.standard_normal(N))}


def core(x, w_words, w_scales, b, v_words, v_scales, c):
    z = mxq(f64(x), 1, "e4m3") @ unpack4(w_words, w_scales)
    z = z.reshape(M, P, F) + f64(b)
    h = z.max(axis=1)
    y = mxq(h, 1, "e4m3") @ unpack_weight(v_words, v_scales, "e4m3")
    return y + f64(c)


def e4m3fn_bytes(y):
    return np.clip(np.asarray(y, np.float64), -448.0, 448.0).astype(np.float32).astype(ml_dtypes.float8_e4m3fn).view(np.uint8)


def e4m3fn_values(b):
    return np.asarray(b, np.uint8).view(ml_dtypes.float8_e4m3fn).astype(np.float64)


def setup_inputs():
    d = draw0()
    x0 = np.asarray(d['x']).astype(np.float64)
    s = (np.max(np.abs(x0), axis=(0,), keepdims=True) / 448.0).astype(np.float32)
    out = {}
    for k, v in d.items():
        if k == 'x':
            out['x_bytes'] = e4m3fn_bytes(x0 / s.astype(np.float64))
            out['x_scale'] = s
        else:
            out[k] = v
    return out


def reference(x_bytes, x_scale, w_words, w_scales, b, v_words, v_scales, c):
    return core(e4m3fn_values(x_bytes) * x_scale.astype(np.float64), w_words, w_scales, b, v_words, v_scales, c)

@@ -1,0 +1,288 @@
+from contextlib import ExitStack
+
+import concourse.mybir as mybir
+from concourse.masks import make_identity
+
+M, K, F, PIECES, N = 1024, 1024, 1024, 3, 1024
+FLOPS = 2 * M * K * PIECES * F + 2 * M * F * N
+
+F32 = mybir.dt.float32
+BF16 = mybir.dt.bfloat16
+I32 = mybir.dt.int32
+U32 = mybir.dt.uint32
+U8 = mybir.dt.uint8
+E4M3 = mybir.dt.float8_e4m3fn
+FP8X4 = mybir.dt.float8_e4m3fn_x4
+FP4X4 = mybir.dt.float4_e2m1fn_x4
+ALU = mybir.AluOpType
+ACT = mybir.ActivationFunctionType
+
+P = 128
+ROWS = 512
+HALVES = M // ROWS
+TILES = F // P
+
+
+def tile_maxout_then_linear_f7_kernel(tc, x_bytes, x_scale, w_words, w_scales, b, v_words, v_scales, c, out):
+    nc = tc.nc
+    with ExitStack() as ctx:
+        keep = ctx.enter_context(tc.tile_pool(name="keep", bufs=1))
+        stage = ctx.enter_context(tc.tile_pool(name="stage", bufs=4))
+        zpool = ctx.enter_context(tc.psum_pool(name="zpool", bufs=6))
+        tpool = ctx.enter_context(tc.psum_pool(name="tpool", bufs=2))
+        ctx.enter_context(tc.manual_schedule())
+
+        xs = keep.tile([P, K], F32, name="xs")
+        nc.scalar.dma_start(out=xs[:], in_=x_scale.rearrange("o k -> (o k)").partition_broadcast(P))
+        braw = keep.tile([P, P], BF16, name="braw")
+        nc.gpsimd.memset(braw[:], 0.0)
+        nc.scalar.dma_start(out=braw[0:24, :], in_=b.rearrange("j (t p) -> (j t) p", p=P))
+        ident = keep.tile([P, P], F32, name="ident")
+        make_identity(nc, ident[:])
+        ws = keep.tile([P, 2, PIECES * F], U8, name="ws", align_bytes=64)
+        nc.vector.memset(ws[:].rearrange("p g n -> p (g n)").bitcast(U32), 0)
+        vs = keep.tile([P, 2, N], U8, name="vs", align_bytes=64)
+        nc.gpsimd.memset(vs[:].rearrange("p g n -> p (g n)").bitcast(U32), 0)
+
+        xb = [keep.tile([P, K], U8, name="xb%d" % i, align_bytes=64) for i in range(8)]
+        wt = [keep.tile([P, 2, PIECES, 512], U8, name="wt%d" % q, align_bytes=64) for q in range(4)]
+        vt = keep.tile([P, 2, 4 * N], U8, name="vt", align_bytes=64)
+        cb = keep.tile([P, N], BF16, name="cb")
+
+        def load_x(i):
+            nc.sync.dma_start(out=xb[i][:], in_=x_bytes[i * P : (i + 1) * P, :])
+
+        def load_w(q):
+            for g in range(2):
+                nc.sync.dma_start(
+                    out=wt[q][:, g].bitcast(I32),
+                    in_=w_words[g].rearrange("p (j n) -> p j n", j=PIECES)[:, :, q * 512 : (q + 1) * 512].bitcast(I32),
+                )
+
+        def load_scales(tile, scales):
+            for q in range(4):
+                nc.sync.dma_start(
+                    out=tile[32 * q : 32 * q + 4].bitcast(I32),
+                    in_=scales[:, 4 * q : 4 * q + 4, :].rearrange("g q n -> q g n").bitcast(I32),
+                )
+
+        load_x(0)
+        load_x(1)
+        load_scales(ws, w_scales)
+        load_w(0)
+        load_x(2)
+        load_x(3)
+        load_w(1)
+        load_x(4)
+        load_w(2)
+        load_x(5)
+        load_w(3)
+        load_x(6)
+        load_x(7)
+        for g in range(2):
+            nc.sync.dma_start(out=vt[:, g].bitcast(I32), in_=v_words[g].rearrange("p n t -> p (n t)").bitcast(I32))
+        load_scales(vs, v_scales)
+        nc.sync.dma_start(out=cb[:], in_=c.partition_broadcast(P))
+
+        xc = [keep.tile([P, 2, ROWS], U32, name="xc%d" % i, align_bytes=64) for i in range(HALVES)]
+        xcs = [keep.tile([P, 2, ROWS], U8, name="xcs%d" % i, align_bytes=64) for i in range(HALVES)]
+        hc = [keep.tile([P, 2, ROWS], U32, name="hc%d" % i, align_bytes=64) for i in range(HALVES)]
+        hcs = [keep.tile([P, 2, ROWS], U8, name="hcs%d" % i, align_bytes=64) for i in range(HALVES)]
+        hp = [[keep.tile([P, 4, ROWS], BF16, name="hp%d%d" % (i, g), align_bytes=64) for g in range(2)] for i in range(HALVES)]
+        bias = keep.tile([P, 24], F32, name="bias")
+        bf32 = keep.tile([P, P], F32, name="bf32")
+
+        xw, xt, xg = {}, {}, {}
+
+        def x_scaled(i):
+            w = stage.tile([P, K], BF16, name="xw", align_bytes=64)
+            nc.vector.tensor_tensor(out=w[:], in0=xb[i][:].bitcast(E4M3), in1=xs[:], op=ALU.mult)
+            xw[i] = w
+
+        def x_turn(i):
+            words = xw[i][:].bitcast(F32)
+            t = tpool.tile([P, 2, 2, P], F32, name="xt")
+            for g in range(2):
+                for u in range(2):
+                    nc.tensor.transpose(t[:, g, u, :], words[:, 256 * g + u : 256 * (g + 1) : 2], ident[:])
+            xt[i] = t
+
+        def x_out(i):
+            a = stage.tile([P, 2, P, 4], BF16, name="xg", align_bytes=64)
+            for g in range(2):
+                nc.scalar.copy(out=a[:, g].rearrange("p m t -> p (m t)").bitcast(F32), in_=xt[i][:, g].rearrange("p u m -> p m u"))
+            xg[i] = a
+
+        def x_quant(i):
+            half, r = i // 4, i % 4
+            for g in range(2):
+                nc.vector.quantize_mx(
+                    out=xc[half][:, g, r * P : (r + 1) * P].bitcast(FP8X4),
+                    scales=xcs[half][:, g, r * P : (r + 1) * P],
+                    in_=xg[i][:, g].rearrange("p m t -> p (m t)"),
+                )
+
+        zs, us, vv, hh = {}, {}, {}, {}
+
+        def z_new(s):
+            zs[s] = []
+            for j in range(PIECES):
+                z = zpool.tile([P, ROWS], F32, name="z")
+                zs[s].append(z)
+
+        def z_mul(s, lo, hi):
+            half, T = s // TILES, s % TILES
+            col = (T % 2) * 256
+            for j in range(PIECES):
+                for g in range(2):
+                    nc.tensor.matmul_mx(
+                        out=zs[s][j][:, lo:hi],
+                        lhsT=wt[T // 2][:, g, j, col : col + 256].bitcast(FP4X4),
+                        lhsT_scale=ws[:, g, j * F + T * P : j * F + (T + 1) * P],
+                        rhs=xc[half][:, g, lo:hi].bitcast(FP8X4),
+                        rhs_scale=xcs[half][:, g, lo:hi],
+                        start=(g == 0),
+                        stop=(g == 1),
+                    )
+
+        def u_out(s):
+            T = s % TILES
+            us[s] = []
+            for j in range(2):
+                u = stage.tile([P, ROWS], BF16, name="u%d" % j, align_bytes=64)
+                nc.scalar.activation(out=u[:], in_=zs[s][j][:], func=ACT.Identity, bias=bias[:, 8 * j + T : 8 * j + T + 1])
+                us[s].append(u)
+
+        def v_max(s):
+            v = stage.tile([P, ROWS], BF16, name="v", align_bytes=64)
+            nc.vector.tensor_tensor(out=v[:], in0=us[s][0][:], in1=us[s][1][:], op=ALU.max)
+            vv[s] = v
+
+        def h_max(s):
+            T = s % TILES
+            h = stage.tile([P, ROWS], BF16, name="h", align_bytes=64)
+            nc.vector.scalar_tensor_tensor(
+                out=h[:], in0=zs[s][2][:], scalar=bias[:, 16 + T : 17 + T], in1=vv[s][:], op0=ALU.add, op1=ALU.max
+            )
+            hh[s] = h
+
+        def h_move(s):
+            half, T = s // TILES, s % TILES
+            g, q = T // 4, T % 4
+            for t in range(4):
+                nc.sync.dma_start(out=hp[half][g][32 * q : 32 * q + 32, t, :], in_=hh[s][t:P:4, :])
+
+        hg = {}
+
+        def h_weave(half, g, r, engine):
+            a = stage.tile([P, P, 4], BF16, name="hg", align_bytes=64)
+            src = hp[half][g][:, :, r * P : (r + 1) * P].rearrange("p t m -> p m t")
+            if engine == "v":
+                nc.vector.tensor_copy(out=a[:], in_=src)
+            else:
+                nc.scalar.copy(out=a[:], in_=src)
+            hg[(half, g, r)] = a
+
+        def h_quant(half, g, r):
+            nc.vector.quantize_mx(
+                out=hc[half][:, g, r * P : (r + 1) * P].bitcast(FP8X4),
+                scales=hcs[half][:, g, r * P : (r + 1) * P],
+                in_=hg[(half, g, r)][:].rearrange("p m t -> p (m t)"),
+            )
+
+        ys, yt = {}, {}
+
+        def y_mul(half, r):
+            for n in range(2):
+                y = zpool.tile([P, ROWS], F32, name="z")
+                for g in range(2):
+                    nc.tensor.matmul_mx(
+                        out=y[:],
+                        lhsT=hc[half][:, g, r * P : (r + 1) * P].bitcast(FP8X4),
+                        lhsT_scale=hcs[half][:, g, r * P : (r + 1) * P],
+                        rhs=vt[:, g, n * 2048 : (n + 1) * 2048].bitcast(FP8X4),
+                        rhs_scale=vs[:, g, n * 512 : (n + 1) * 512],
+                        start=(g == 0),
+                        stop=(g == 1),
+                    )
+                ys[(half, r, n)] = y
+
+        def y_out(half, r, how):
+            o = stage.tile([P, N], F32, name="yt")
+            m0 = half * ROWS + r * P
+            for n in range(2):
+                cols = slice(n * 512, (n + 1) * 512)
+                y = ys[(half, r, n)]
+                if how[n] == "v":
+                    nc.vector.tensor_tensor(out=o[:, cols], in0=y[:], in1=cb[:, cols], op=ALU.add)
+                else:
+                    e = stage.tile([P, 512], F32, name="ye")
+                    nc.scalar.copy(out=e[:], in_=y[:])
+                    nc.gpsimd.tensor_tensor(out=o[:, cols], in0=e[:], in1=cb[:, cols], op=ALU.add)
+            nc.sync.dma_start(out=out[m0 : m0 + P, :], in_=o[:])
+
+        z_new(0)
+        z_new(1)
+        x_scaled(0)
+        x_turn(0)
+        x_out(0)
+        x_scaled(1)
+        x_quant(0)
+        x_turn(1)
+        x_out(1)
+        z_mul(0, 0, P)
+        z_mul(1, 0, P)
+        x_scaled(2)
+        x_quant(1)
+        x_turn(2)
+        x_out(2)
+        z_mul(0, P, 2 * P)
+        z_mul(1, P, 2 * P)
+        x_scaled(3)
+        x_quant(2)
+        x_turn(3)
+        x_out(3)
+        z_mul(0, 2 * P, 3 * P)
+        z_mul(1, 2 * P, 3 * P)
+        nc.vector.tensor_copy(out=bf32[:], in_=braw[:])
+        bps = tpool.tile([P, P], F32, name="xt")
+        nc.tensor.transpose(bps[:], bf32[:], ident[:])
+        x_quant(3)
+        nc.vector.tensor_copy(out=bias[:], in_=bps[:, 0:24])
+        z_mul(0, 3 * P, 4 * P)
+        z_mul(1, 3 * P, 4 * P)
+        x_scaled(4)
+
+        for s in range(16):
+            if s >= 2:
+                z_new(s)
+                z_mul(s, 0, ROWS)
+            u_out(s)
+            v_max(s)
+            if s in (1, 3, 5):
+                x_scaled(4 + (s + 1) // 2)
+            if 8 <= s:
+                h_weave(0, (s - 8) // 4, s % 4, "v")
+            h_max(s)
+            h_move(s)
+            if 8 <= s:
+                h_quant(0, (s - 8) // 4, s % 4)
+            if s in (1, 2, 4, 6):
+                i = 4 + s // 2
+                x_turn(i)
+                x_out(i)
+                x_quant(i)
+            if s >= 14:
+                h_weave(1, 0, 2 * (s - 14), "s")
+                h_weave(1, 0, 2 * (s - 14) + 1, "s")
+
+        for r in range(4):
+            y_mul(0, r)
+            y_out(0, r, "vs")
+            h_quant(1, 0, r)
+        for r in range(4):
+            h_weave(1, 1, r, "vs"[r % 2])
+            h_quant(1, 1, r)
+        for r in range(4):
+            y_mul(1, r)
+            y_out(1, r, "vs" if r < 3 else "vv")

@@ -28,15 +28,18 @@ def tile_maxout_then_linear_f7_kernel(tc, x_bytes, x_scale, w_words, w_scales, b
     with ExitStack() as ctx:
         keep = ctx.enter_context(tc.tile_pool(name="keep", bufs=1))
         stage = ctx.enter_context(tc.tile_pool(name="stage", bufs=4))
+        deep = ctx.enter_context(tc.tile_pool(name="deep", bufs=8))
         zpool = ctx.enter_context(tc.psum_pool(name="zpool", bufs=6))
         tpool = ctx.enter_context(tc.psum_pool(name="tpool", bufs=2))
         ctx.enter_context(tc.manual_schedule())
 
-        xs = keep.tile([P, K], F32, name="xs")
-        nc.scalar.dma_start(out=xs[:], in_=x_scale.rearrange("o k -> (o k)").partition_broadcast(P))
+        sc = keep.tile([P, 2, 2, 2], F32, name="sc")
+        nc.gpsimd.dma_start(
+            out=sc[:].rearrange("p g u e -> p g (u e)"), in_=x_scale.rearrange("o (g p t) -> p (o g) t", g=2, t=4)
+        )
         braw = keep.tile([P, P], BF16, name="braw")
         nc.gpsimd.memset(braw[:], 0.0)
-        nc.scalar.dma_start(out=braw[0:24, :], in_=b.rearrange("j (t p) -> (j t) p", p=P))
+        nc.gpsimd.dma_start(out=braw[0:24, :], in_=b.rearrange("j (t p) -> (j t) p", p=P))
         ident = keep.tile([P, P], F32, name="ident")
         make_identity(nc, ident[:])
         ws = keep.tile([P, 2, PIECES * F], U8, name="ws", align_bytes=64)
@@ -44,13 +47,20 @@ def tile_maxout_then_linear_f7_kernel(tc, x_bytes, x_scale, w_words, w_scales, b
         vs = keep.tile([P, 2, N], U8, name="vs", align_bytes=64)
         nc.gpsimd.memset(vs[:].rearrange("p g n -> p (g n)").bitcast(U32), 0)
 
-        xb = [keep.tile([P, K], U8, name="xb%d" % i, align_bytes=64) for i in range(8)]
+        xb4 = [keep.tile([P, 4, K], U8, name="xb%d" % i, align_bytes=64) for i in range(2)]
+        xb = [xb4[i // 4][:, i % 4] for i in range(8)]
         wt = [keep.tile([P, 2, PIECES, 512], U8, name="wt%d" % q, align_bytes=64) for q in range(4)]
         vt = keep.tile([P, 2, 4 * N], U8, name="vt", align_bytes=64)
-        cb = keep.tile([P, N], BF16, name="cb")
+        crow = keep.tile([P, N], BF16, name="crow")
+        nc.gpsimd.memset(crow[:], 0.0)
+        ones = keep.tile([P, P], BF16, name="ones")
+        nc.gpsimd.memset(ones[:], 1.0)
+        cb = keep.tile([P, N], F32, name="cb")
 
-        def load_x(i):
-            nc.sync.dma_start(out=xb[i][:], in_=x_bytes[i * P : (i + 1) * P, :])
+        def load_x(lo, hi):
+            nc.sync.dma_start(
+                out=xb4[lo // 4][:, lo % 4 : lo % 4 + hi - lo], in_=x_bytes[lo * P : hi * P, :].rearrange("(r p) k -> p r k", p=P)
+            )
 
         def load_w(q):
             for g in range(2):
@@ -66,23 +76,18 @@ def tile_maxout_then_linear_f7_kernel(tc, x_bytes, x_scale, w_words, w_scales, b
                     in_=scales[:, 4 * q : 4 * q + 4, :].rearrange("g q n -> q g n").bitcast(I32),
                 )
 
-        load_x(0)
-        load_x(1)
+        load_x(0, 1)
+        load_x(1, 2)
         load_scales(ws, w_scales)
+        load_x(2, 4)
         load_w(0)
-        load_x(2)
-        load_x(3)
-        load_w(1)
-        load_x(4)
-        load_w(2)
-        load_x(5)
-        load_w(3)
-        load_x(6)
-        load_x(7)
+        load_x(4, 8)
+        for q in range(1, 4):
+            load_w(q)
         for g in range(2):
             nc.sync.dma_start(out=vt[:, g].bitcast(I32), in_=v_words[g].rearrange("p n t -> p (n t)").bitcast(I32))
         load_scales(vs, v_scales)
-        nc.sync.dma_start(out=cb[:], in_=c.partition_broadcast(P))
+        nc.gpsimd.dma_start(out=crow[0:1, :], in_=c.unsqueeze(0))
 
         xc = [keep.tile([P, 2, ROWS], U32, name="xc%d" % i, align_bytes=64) for i in range(HALVES)]
         xcs = [keep.tile([P, 2, ROWS], U8, name="xcs%d" % i, align_bytes=64) for i in range(HALVES)]
@@ -94,9 +99,12 @@ def tile_maxout_then_linear_f7_kernel(tc, x_bytes, x_scale, w_words, w_scales, b
 
         xw, xt, xg = {}, {}, {}
 
-        def x_scaled(i):
-            w = stage.tile([P, K], BF16, name="xw", align_bytes=64)
-            nc.vector.tensor_tensor(out=w[:], in0=xb[i][:].bitcast(E4M3), in1=xs[:], op=ALU.mult)
+        def x_cast(i, engine):
+            w = deep.tile([P, K], BF16, name="xw", align_bytes=64)
+            if engine == "v":
+                nc.vector.tensor_copy(out=w[:], in_=xb[i].bitcast(E4M3))
+            else:
+                nc.scalar.copy(out=w[:], in_=xb[i].bitcast(E4M3))
             xw[i] = w
 
         def x_turn(i):
@@ -107,15 +115,22 @@ def tile_maxout_then_linear_f7_kernel(tc, x_bytes, x_scale, w_words, w_scales, b
                     nc.tensor.transpose(t[:, g, u, :], words[:, 256 * g + u : 256 * (g + 1) : 2], ident[:])
             xt[i] = t
 
-        def x_out(i):
-            a = stage.tile([P, 2, P, 4], BF16, name="xg", align_bytes=64)
-            for g in range(2):
-                nc.scalar.copy(out=a[:, g].rearrange("p m t -> p (m t)").bitcast(F32), in_=xt[i][:, g].rearrange("p u m -> p m u"))
-            xg[i] = a
+        def x_out(i, g):
+            if g == 0:
+                a = stage.tile([P, 2, P, 4], BF16, name="xg", align_bytes=64)
+                xg[i] = a
+            a = xg[i]
+            if True:
+                nc.vector.tensor_tensor(
+                    out=a[:, g].rearrange("p m (u e) -> p m u e", u=2),
+                    in0=xt[i][:, g].bitcast(BF16).rearrange("p u (m e) -> p m u e", e=2),
+                    in1=sc[:, g].unsqueeze(1).to_broadcast([P, P, 2, 2]),
+                    op=ALU.mult,
+                )
 
-        def x_quant(i):
+        def x_quant(i, g):
             half, r = i // 4, i % 4
-            for g in range(2):
+            if True:
                 nc.vector.quantize_mx(
                     out=xc[half][:, g, r * P : (r + 1) * P].bitcast(FP8X4),
                     scales=xcs[half][:, g, r * P : (r + 1) * P],
@@ -145,10 +160,10 @@ def tile_maxout_then_linear_f7_kernel(tc, x_bytes, x_scale, w_words, w_scales, b
                         stop=(g == 1),
                     )
 
-        def u_out(s):
+        def u_out(s, pieces=2):
             T = s % TILES
             us[s] = []
-            for j in range(2):
+            for j in range(pieces):
                 u = stage.tile([P, ROWS], BF16, name="u%d" % j, align_bytes=64)
                 nc.scalar.activation(out=u[:], in_=zs[s][j][:], func=ACT.Identity, bias=bias[:, 8 * j + T : 8 * j + T + 1])
                 us[s].append(u)
@@ -161,10 +176,13 @@ def tile_maxout_then_linear_f7_kernel(tc, x_bytes, x_scale, w_words, w_scales, b
         def h_max(s):
             T = s % TILES
             h = stage.tile([P, ROWS], BF16, name="h", align_bytes=64)
+            hh[s] = h
+            if len(us[s]) == 3:
+                nc.vector.tensor_tensor(out=h[:], in0=us[s][2][:], in1=vv[s][:], op=ALU.max)
+                return
             nc.vector.scalar_tensor_tensor(
                 out=h[:], in0=zs[s][2][:], scalar=bias[:, 16 + T : 17 + T], in1=vv[s][:], op0=ALU.add, op1=ALU.max
             )
-            hh[s] = h
 
         def h_move(s):
             half, T = s // TILES, s % TILES
@@ -175,7 +193,7 @@ def tile_maxout_then_linear_f7_kernel(tc, x_bytes, x_scale, w_words, w_scales, b
         hg = {}
 
         def h_weave(half, g, r, engine):
-            a = stage.tile([P, P, 4], BF16, name="hg", align_bytes=64)
+            a = deep.tile([P, P, 4], BF16, name="hg", align_bytes=64)
             src = hp[half][g][:, :, r * P : (r + 1) * P].rearrange("p t m -> p m t")
             if engine == "v":
                 nc.vector.tensor_copy(out=a[:], in_=src)
@@ -207,82 +225,122 @@ def tile_maxout_then_linear_f7_kernel(tc, x_bytes, x_scale, w_words, w_scales, b
                     )
                 ys[(half, r, n)] = y
 
-        def y_out(half, r, how):
-            o = stage.tile([P, N], F32, name="yt")
+        def y_out(half, r, n, how):
+            if n == 0:
+                o = deep.tile([P, N], F32, name="yt")
+                yt[(half, r)] = o
+            o = yt[(half, r)]
+            cols = slice(n * 512, (n + 1) * 512)
+            y = ys[(half, r, n)]
+            if how == "v":
+                nc.vector.tensor_tensor(out=o[:, cols], in0=y[:], in1=cb[:, cols], op=ALU.add)
+            else:
+                e = stage.tile([P, 512], F32, name="ye")
+                nc.scalar.copy(out=e[:], in_=y[:])
+                nc.gpsimd.tensor_tensor(out=o[:, cols], in0=e[:], in1=cb[:, cols], op=ALU.add)
+
+        def y_store(half, r, lo=0, hi=N):
             m0 = half * ROWS + r * P
-            for n in range(2):
-                cols = slice(n * 512, (n + 1) * 512)
-                y = ys[(half, r, n)]
-                if how[n] == "v":
-                    nc.vector.tensor_tensor(out=o[:, cols], in0=y[:], in1=cb[:, cols], op=ALU.add)
-                else:
-                    e = stage.tile([P, 512], F32, name="ye")
-                    nc.scalar.copy(out=e[:], in_=y[:])
-                    nc.gpsimd.tensor_tensor(out=o[:, cols], in0=e[:], in1=cb[:, cols], op=ALU.add)
-            nc.sync.dma_start(out=out[m0 : m0 + P, :], in_=o[:])
+            nc.sync.dma_start(out=out[m0 : m0 + P, lo:hi], in_=yt[(half, r)][:, lo:hi])
 
         z_new(0)
         z_new(1)
-        x_scaled(0)
+
+        def head_mul(r):
+            z_mul(0, r * P, (r + 1) * P)
+            z_mul(1, r * P, (r + 1) * P)
+
+        def x_both(f, i):
+            f(i, 0)
+            f(i, 1)
+
+        x_cast(0, "v")
+        x_cast(1, "s")
         x_turn(0)
-        x_out(0)
-        x_scaled(1)
-        x_quant(0)
+        x_cast(2, "s")
+        x_both(x_out, 0)
         x_turn(1)
-        x_out(1)
-        z_mul(0, 0, P)
-        z_mul(1, 0, P)
-        x_scaled(2)
-        x_quant(1)
+        x_both(x_quant, 0)
+        x_both(x_out, 1)
+        x_cast(3, "s")
         x_turn(2)
-        x_out(2)
-        z_mul(0, P, 2 * P)
-        z_mul(1, P, 2 * P)
-        x_scaled(3)
-        x_quant(2)
+        head_mul(0)
+        x_out(2, 0)
+        x_both(x_quant, 1)
+        x_out(2, 1)
+        x_cast(4, "s")
         x_turn(3)
-        x_out(3)
-        z_mul(0, 2 * P, 3 * P)
-        z_mul(1, 2 * P, 3 * P)
+        head_mul(1)
+        x_out(3, 0)
+        x_both(x_quant, 2)
+        x_out(3, 1)
         nc.vector.tensor_copy(out=bf32[:], in_=braw[:])
+        x_turn(4)
+        head_mul(2)
         bps = tpool.tile([P, P], F32, name="xt")
         nc.tensor.transpose(bps[:], bf32[:], ident[:])
-        x_quant(3)
+        x_both(x_quant, 3)
         nc.vector.tensor_copy(out=bias[:], in_=bps[:, 0:24])
-        z_mul(0, 3 * P, 4 * P)
-        z_mul(1, 3 * P, 4 * P)
-        x_scaled(4)
+        head_mul(3)
+        for i in (5, 6, 7):
+            x_cast(i, "s")
+        x_both(x_out, 4)
+        x_both(x_quant, 4)
 
+        pend = []
         for s in range(16):
             if s >= 2:
                 z_new(s)
                 z_mul(s, 0, ROWS)
-            u_out(s)
+            u_out(s, 3 if s == 15 else 2)
+            ready, pend = pend, []
+            if s in (0, 2, 4):
+                x_turn(5 + s // 2)
             v_max(s)
-            if s in (1, 3, 5):
-                x_scaled(4 + (s + 1) // 2)
+            if 1 <= s <= 6:
+                i, g = 5 + (s - 1) // 2, (s - 1) % 2
+                x_out(i, g)
             if 8 <= s:
-                h_weave(0, (s - 8) // 4, s % 4, "v")
+                pend.append((0, (s - 8) // 4, s % 4))
+                h_weave(*pend[-1], "v")
+            if s == 14:
+                pend.append((1, 0, 0))
+                h_weave(1, 0, 0, "s")
             h_max(s)
             h_move(s)
-            if 8 <= s:
-                h_quant(0, (s - 8) // 4, s % 4)
-            if s in (1, 2, 4, 6):
-                i = 4 + s // 2
-                x_turn(i)
-                x_out(i)
-                x_quant(i)
-            if s >= 14:
-                h_weave(1, 0, 2 * (s - 14), "s")
-                h_weave(1, 0, 2 * (s - 14) + 1, "s")
-
+            for q in ready:
+                h_quant(*q)
+            if 1 <= s <= 6:
+                x_quant(i, g)
+            if s == 8:
+                for n in range(2):
+                    cps = tpool.tile([P, 512], F32, name="xt")
+                    nc.tensor.matmul(cps[:], lhsT=ones[:], rhs=crow[:, n * 512 : (n + 1) * 512], start=True, stop=True)
+                    nc.scalar.copy(out=cb[:, n * 512 : (n + 1) * 512], in_=cps[:])
+        for q in pend:
+            h_quant(*q)
+        h_weave(1, 0, 1, "s")
+        h_weave(1, 0, 2, "s")
         for r in range(4):
             y_mul(0, r)
-            y_out(0, r, "vs")
-            h_quant(1, 0, r)
+            y_out(0, r, 0, "v")
+            y_out(0, r, 1, "v" if r == 3 else "s")
+            y_store(0, r)
+            if r == 0:
+                h_weave(1, 0, 3, "s")
+                h_quant(1, 0, 1)
+                h_quant(1, 0, 2)
+            if r == 2:
+                h_quant(1, 0, 3)
         for r in range(4):
             h_weave(1, 1, r, "vs"[r % 2])
+        for r in range(4):
             h_quant(1, 1, r)
         for r in range(4):
             y_mul(1, r)
-            y_out(1, r, "vs" if r < 3 else "vv")
+            y_out(1, r, 0, "v")
+            y_out(1, r, 1, "v" if r == 3 else "s")
+            if r < 3:
+                y_store(1, r)
+        y_store(1, 3, 0, 512)
+        y_store(1, 3, 512, N)

@@ -43,7 +43,8 @@ def tile_maxout_then_linear_f7_kernel(tc, x_bytes, x_scale, w_words, w_scales, b
         ident = keep.tile([P, P], F32, name="ident")
         make_identity(nc, ident[:])
         ws = keep.tile([P, 2, PIECES * F], U8, name="ws", align_bytes=64)
-        nc.vector.memset(ws[:].rearrange("p g n -> p (g n)").bitcast(U32), 0)
+        nc.vector.memset(ws[:, 0].bitcast(U32), 0)
+        nc.gpsimd.memset(ws[:, 1].bitcast(U32), 0)
         vs = keep.tile([P, 2, N], U8, name="vs", align_bytes=64)
         nc.gpsimd.memset(vs[:].rearrange("p g n -> p (g n)").bitcast(U32), 0)
 
@@ -81,9 +82,11 @@ def tile_maxout_then_linear_f7_kernel(tc, x_bytes, x_scale, w_words, w_scales, b
         load_scales(ws, w_scales)
         load_x(2, 4)
         load_w(0)
-        load_x(4, 8)
-        for q in range(1, 4):
-            load_w(q)
+        load_x(4, 6)
+        load_w(1)
+        load_x(6, 8)
+        load_w(2)
+        load_w(3)
         for g in range(2):
             nc.sync.dma_start(out=vt[:, g].bitcast(I32), in_=v_words[g].rearrange("p n t -> p (n t)").bitcast(I32))
         load_scales(vs, v_scales)
@@ -102,7 +105,8 @@ def tile_maxout_then_linear_f7_kernel(tc, x_bytes, x_scale, w_words, w_scales, b
         def x_cast(i, engine):
             w = deep.tile([P, K], BF16, name="xw", align_bytes=64)
             if engine == "v":
-                nc.vector.tensor_copy(out=w[:], in_=xb[i].bitcast(E4M3))
+                for g in range(2):
+                    nc.vector.tensor_copy(out=w[:, g * 512 : (g + 1) * 512], in_=xb[i][:, g * 512 : (g + 1) * 512].bitcast(E4M3))
             else:
                 nc.scalar.copy(out=w[:], in_=xb[i].bitcast(E4M3))
             xw[i] = w
@@ -210,20 +214,20 @@ def tile_maxout_then_linear_f7_kernel(tc, x_bytes, x_scale, w_words, w_scales, b
 
         ys, yt = {}, {}
 
-        def y_mul(half, r):
+        def y_mul(half, r, g):
             for n in range(2):
-                y = zpool.tile([P, ROWS], F32, name="z")
-                for g in range(2):
-                    nc.tensor.matmul_mx(
-                        out=y[:],
-                        lhsT=hc[half][:, g, r * P : (r + 1) * P].bitcast(FP8X4),
-                        lhsT_scale=hcs[half][:, g, r * P : (r + 1) * P],
-                        rhs=vt[:, g, n * 2048 : (n + 1) * 2048].bitcast(FP8X4),
-                        rhs_scale=vs[:, g, n * 512 : (n + 1) * 512],
-                        start=(g == 0),
-                        stop=(g == 1),
-                    )
-                ys[(half, r, n)] = y
+                if g == 0:
+                    y = zpool.tile([P, ROWS], F32, name="z")
+                    ys[(half, r, n)] = y
+                nc.tensor.matmul_mx(
+                    out=ys[(half, r, n)][:],
+                    lhsT=hc[half][:, g, r * P : (r + 1) * P].bitcast(FP8X4),
+                    lhsT_scale=hcs[half][:, g, r * P : (r + 1) * P],
+                    rhs=vt[:, g, n * 2048 : (n + 1) * 2048].bitcast(FP8X4),
+                    rhs_scale=vs[:, g, n * 512 : (n + 1) * 512],
+                    start=(g == 0),
+                    stop=(g == 1),
+                )
 
         def y_out(half, r, n, how):
             if n == 0:
@@ -260,8 +264,12 @@ def tile_maxout_then_linear_f7_kernel(tc, x_bytes, x_scale, w_words, w_scales, b
         x_cast(2, "s")
         x_both(x_out, 0)
         x_turn(1)
+        nc.vector.tensor_copy(out=bf32[:], in_=braw[:])
+        bps = zs[1][2][:, 3 * P : 4 * P]
+        nc.tensor.transpose(bps, bf32[:], ident[:])
         x_both(x_quant, 0)
         x_both(x_out, 1)
+        nc.vector.tensor_copy(out=bias[:], in_=bps[:, 0:24])
         x_cast(3, "s")
         x_turn(2)
         head_mul(0)
@@ -271,16 +279,12 @@ def tile_maxout_then_linear_f7_kernel(tc, x_bytes, x_scale, w_words, w_scales, b
         x_cast(4, "s")
         x_turn(3)
         head_mul(1)
+        x_turn(4)
         x_out(3, 0)
         x_both(x_quant, 2)
         x_out(3, 1)
-        nc.vector.tensor_copy(out=bf32[:], in_=braw[:])
-        x_turn(4)
         head_mul(2)
-        bps = tpool.tile([P, P], F32, name="xt")
-        nc.tensor.transpose(bps[:], bf32[:], ident[:])
         x_both(x_quant, 3)
-        nc.vector.tensor_copy(out=bias[:], in_=bps[:, 0:24])
         head_mul(3)
         for i in (5, 6, 7):
             x_cast(i, "s")
@@ -294,8 +298,8 @@ def tile_maxout_then_linear_f7_kernel(tc, x_bytes, x_scale, w_words, w_scales, b
                 z_mul(s, 0, ROWS)
             u_out(s, 3 if s == 15 else 2)
             ready, pend = pend, []
-            if s in (0, 2, 4):
-                x_turn(5 + s // 2)
+            if s in (0, 1, 3):
+                x_turn(5 + (s + 1) // 2)
             v_max(s)
             if 1 <= s <= 6:
                 i, g = 5 + (s - 1) // 2, (s - 1) % 2
@@ -317,30 +321,47 @@ def tile_maxout_then_linear_f7_kernel(tc, x_bytes, x_scale, w_words, w_scales, b
                     cps = tpool.tile([P, 512], F32, name="xt")
                     nc.tensor.matmul(cps[:], lhsT=ones[:], rhs=crow[:, n * 512 : (n + 1) * 512], start=True, stop=True)
                     nc.scalar.copy(out=cb[:, n * 512 : (n + 1) * 512], in_=cps[:])
+        def y_done(half, r, n, how):
+            y_out(half, r, n, how)
+            y_store(half, r, n * 512, (n + 1) * 512)
+
+        y_mul(0, 0, 0)
+        y_mul(0, 0, 1)
+        y_done(0, 0, 0, "v")
+        y_done(0, 0, 1, "s")
+        h_weave(1, 0, 1, "s")
         for q in pend:
             h_quant(*q)
-        h_weave(1, 0, 1, "s")
+        y_mul(0, 1, 0)
+        y_mul(0, 1, 1)
+        y_done(0, 1, 0, "v")
+        y_done(0, 1, 1, "s")
+        h_quant(1, 0, 1)
         h_weave(1, 0, 2, "s")
+        y_mul(0, 2, 0)
+        y_mul(0, 2, 1)
+        y_done(0, 2, 0, "v")
+        y_done(0, 2, 1, "v")
+        h_weave(1, 0, 3, "s")
+        y_mul(0, 3, 0)
+        y_mul(0, 3, 1)
+        h_quant(1, 0, 2)
+        y_done(0, 3, 0, "v")
+        h_quant(1, 0, 3)
+        for r in range(3):
+            y_mul(1, r, 0)
+        h_weave(1, 1, 0, "v")
+        h_weave(1, 1, 1, "s")
+        h_weave(1, 1, 2, "v")
+        h_quant(1, 1, 0)
+        h_weave(1, 1, 3, "s")
+        h_quant(1, 1, 1)
+        h_quant(1, 1, 2)
+        y_done(0, 3, 1, "v")
+        h_quant(1, 1, 3)
         for r in range(4):
-            y_mul(0, r)
-            y_out(0, r, 0, "v")
-            y_out(0, r, 1, "v" if r == 3 else "s")
-            y_store(0, r)
-            if r == 0:
-                h_weave(1, 0, 3, "s")
-                h_quant(1, 0, 1)
-                h_quant(1, 0, 2)
-            if r == 2:
-                h_quant(1, 0, 3)
-        for r in range(4):
-            h_weave(1, 1, r, "vs"[r % 2])
-        for r in range(4):
-            h_quant(1, 1, r)
-        for r in range(4):
-            y_mul(1, r)
-            y_out(1, r, 0, "v")
-            y_out(1, r, 1, "v" if r == 3 else "s")
-            if r < 3:
-                y_store(1, r)
-        y_store(1, 3, 0, 512)
-        y_store(1, 3, 512, N)
+            if r == 3:
+                y_mul(1, 3, 0)
+            y_mul(1, r, 1)
+            for n in range(2):
+                y_done(1, r, n, "s" if (r, n) in ((0, 1), (1, 1), (2, 1)) else "v")

@@ -34,17 +34,17 @@ def tile_maxout_then_linear_f7_kernel(tc, x_bytes, x_scale, w_words, w_scales, b
         ctx.enter_context(tc.manual_schedule())
 
         sc = keep.tile([P, 2, 2, 2], F32, name="sc")
-        nc.gpsimd.dma_start(
+        nc.scalar.dma_start(
             out=sc[:].rearrange("p g u e -> p g (u e)"), in_=x_scale.rearrange("o (g p t) -> p (o g) t", g=2, t=4)
         )
-        braw = keep.tile([P, P], BF16, name="braw")
-        nc.gpsimd.memset(braw[:], 0.0)
-        nc.gpsimd.dma_start(out=braw[0:24, :], in_=b.rearrange("j (t p) -> (j t) p", p=P))
         ident = keep.tile([P, P], F32, name="ident")
         make_identity(nc, ident[:])
+        braw = keep.tile([P, P], BF16, name="braw")
+        warm = keep.tile([P, 512], BF16, name="warm")
+        nc.vector.memset(warm[:], 0.0)
+        nc.gpsimd.memset(braw[:], 0.0)
         ws = keep.tile([P, 2, PIECES * F], U8, name="ws", align_bytes=64)
-        nc.vector.memset(ws[:, 0].bitcast(U32), 0)
-        nc.gpsimd.memset(ws[:, 1].bitcast(U32), 0)
+        nc.vector.memset(ws[:].rearrange("p g n -> p (g n)").bitcast(U32), 0)
         vs = keep.tile([P, 2, N], U8, name="vs", align_bytes=64)
         nc.gpsimd.memset(vs[:].rearrange("p g n -> p (g n)").bitcast(U32), 0)
 
@@ -78,10 +78,10 @@ def tile_maxout_then_linear_f7_kernel(tc, x_bytes, x_scale, w_words, w_scales, b
                 )
 
         load_x(0, 1)
-        load_x(1, 2)
+        load_x(1, 4)
         load_scales(ws, w_scales)
-        load_x(2, 4)
         load_w(0)
+        nc.sync.dma_start(out=braw[0:24, :], in_=b.rearrange("j (t p) -> (j t) p", p=P))
         load_x(4, 6)
         load_w(1)
         load_x(6, 8)
@@ -90,7 +90,7 @@ def tile_maxout_then_linear_f7_kernel(tc, x_bytes, x_scale, w_words, w_scales, b
         for g in range(2):
             nc.sync.dma_start(out=vt[:, g].bitcast(I32), in_=v_words[g].rearrange("p n t -> p (n t)").bitcast(I32))
         load_scales(vs, v_scales)
-        nc.gpsimd.dma_start(out=crow[0:1, :], in_=c.unsqueeze(0))
+        nc.sync.dma_start(out=crow[0:1, :], in_=c.unsqueeze(0))
 
         xc = [keep.tile([P, 2, ROWS], U32, name="xc%d" % i, align_bytes=64) for i in range(HALVES)]
         xcs = [keep.tile([P, 2, ROWS], U8, name="xcs%d" % i, align_bytes=64) for i in range(HALVES)]
@@ -217,7 +217,10 @@ def tile_maxout_then_linear_f7_kernel(tc, x_bytes, x_scale, w_words, w_scales, b
         def y_mul(half, r, g):
             for n in range(2):
                 if g == 0:
-                    y = zpool.tile([P, ROWS], F32, name="z")
+                    if r == 3:
+                        y = tpool.tile([P, ROWS], F32, name="xt")
+                    else:
+                        y = zpool.tile([P, ROWS], F32, name="z")
                     ys[(half, r, n)] = y
                 nc.tensor.matmul_mx(
                     out=ys[(half, r, n)][:],
@@ -258,36 +261,43 @@ def tile_maxout_then_linear_f7_kernel(tc, x_bytes, x_scale, w_words, w_scales, b
             f(i, 0)
             f(i, 1)
 
+        def keep_warm(times):
+            for i in range(times):
+                nc.tensor.matmul(zs[1][2][:], lhsT=warm[:, 0:P], rhs=warm[:], start=True, stop=True)
+
+        keep_warm(5)
         x_cast(0, "v")
         x_cast(1, "s")
         x_turn(0)
+        keep_warm(2)
         x_cast(2, "s")
         x_both(x_out, 0)
         x_turn(1)
-        nc.vector.tensor_copy(out=bf32[:], in_=braw[:])
-        bps = zs[1][2][:, 3 * P : 4 * P]
-        nc.tensor.transpose(bps, bf32[:], ident[:])
+        keep_warm(1)
         x_both(x_quant, 0)
         x_both(x_out, 1)
-        nc.vector.tensor_copy(out=bias[:], in_=bps[:, 0:24])
         x_cast(3, "s")
         x_turn(2)
         head_mul(0)
         x_out(2, 0)
         x_both(x_quant, 1)
         x_out(2, 1)
+        nc.scalar.copy(out=bf32[:], in_=braw[:])
         x_cast(4, "s")
         x_turn(3)
         head_mul(1)
         x_turn(4)
+        bps = zs[1][2][:, 3 * P : 4 * P]
+        nc.tensor.transpose(bps, bf32[:], ident[:])
         x_out(3, 0)
+        x_cast(5, "s")
+        nc.scalar.copy(out=bias[:], in_=bps[:, 0:24])
         x_both(x_quant, 2)
         x_out(3, 1)
         head_mul(2)
         x_both(x_quant, 3)
         head_mul(3)
-        for i in (5, 6, 7):
-            x_cast(i, "s")
+        x_cast(6, "s")
         x_both(x_out, 4)
         x_both(x_quant, 4)
 
@@ -297,9 +307,11 @@ def tile_maxout_then_linear_f7_kernel(tc, x_bytes, x_scale, w_words, w_scales, b
                 z_new(s)
                 z_mul(s, 0, ROWS)
             u_out(s, 3 if s == 15 else 2)
+            if s == 1:
+                x_cast(7, "s")
             ready, pend = pend, []
-            if s in (0, 1, 3):
-                x_turn(5 + (s + 1) // 2)
+            if s in (0, 1, 4):
+                x_turn((5, 6, 0, 0, 7)[s])
             v_max(s)
             if 1 <= s <= 6:
                 i, g = 5 + (s - 1) // 2, (s - 1) % 2
@@ -325,43 +337,43 @@ def tile_maxout_then_linear_f7_kernel(tc, x_bytes, x_scale, w_words, w_scales, b
             y_out(half, r, n, how)
             y_store(half, r, n * 512, (n + 1) * 512)
 
-        y_mul(0, 0, 0)
-        y_mul(0, 0, 1)
+        for q in pend:
+            h_quant(*q)
+        for r in range(4):
+            y_mul(0, r, 0)
+            y_mul(0, r, 1)
         y_done(0, 0, 0, "v")
         y_done(0, 0, 1, "s")
         h_weave(1, 0, 1, "s")
-        for q in pend:
-            h_quant(*q)
-        y_mul(0, 1, 0)
-        y_mul(0, 1, 1)
         y_done(0, 1, 0, "v")
         y_done(0, 1, 1, "s")
-        h_quant(1, 0, 1)
         h_weave(1, 0, 2, "s")
-        y_mul(0, 2, 0)
-        y_mul(0, 2, 1)
+        h_quant(1, 0, 1)
         y_done(0, 2, 0, "v")
-        y_done(0, 2, 1, "v")
+        y_done(0, 2, 1, "s")
         h_weave(1, 0, 3, "s")
-        y_mul(0, 3, 0)
-        y_mul(0, 3, 1)
-        h_quant(1, 0, 2)
         y_done(0, 3, 0, "v")
-        h_quant(1, 0, 3)
-        for r in range(3):
-            y_mul(1, r, 0)
         h_weave(1, 1, 0, "v")
         h_weave(1, 1, 1, "s")
-        h_weave(1, 1, 2, "v")
+        h_quant(1, 0, 2)
         h_quant(1, 1, 0)
-        h_weave(1, 1, 3, "s")
-        h_quant(1, 1, 1)
-        h_quant(1, 1, 2)
+        h_weave(1, 1, 2, "s")
         y_done(0, 3, 1, "v")
+        h_weave(1, 1, 3, "s")
+        for r in range(3):
+            y_mul(1, r, 0)
+        h_quant(1, 1, 1)
+        h_quant(1, 0, 3)
+        y_mul(1, 0, 1)
+        y_mul(1, 1, 1)
+        y_mul(1, 3, 0)
+        y_out(1, 0, 0, "v")
+        h_quant(1, 1, 2)
+        y_mul(1, 2, 1)
+        y_out(1, 0, 1, "s")
         h_quant(1, 1, 3)
-        for r in range(4):
-            if r == 3:
-                y_mul(1, 3, 0)
-            y_mul(1, r, 1)
-            for n in range(2):
-                y_done(1, r, n, "s" if (r, n) in ((0, 1), (1, 1), (2, 1)) else "v")
+        y_mul(1, 3, 1)
+        for r, n, how in ((1, 0, "v"), (1, 1, "s"), (2, 0, "v"), (2, 1, "v"), (3, 0, "v"), (3, 1, "v")):
+            y_out(1, r, n, how)
+        for r, n in ((0, 0), (1, 0), (0, 1), (2, 0), (2, 1), (1, 1), (3, 0), (3, 1)):
+            y_store(1, r, n * 512, (n + 1) * 512)

@@ -52,11 +52,7 @@ def tile_maxout_then_linear_f7_kernel(tc, x_bytes, x_scale, w_words, w_scales, b
         xb = [xb4[i // 4][:, i % 4] for i in range(8)]
         wt = [keep.tile([P, 2, PIECES, 512], U8, name="wt%d" % q, align_bytes=64) for q in range(4)]
         vt = keep.tile([P, 2, 4 * N], U8, name="vt", align_bytes=64)
-        crow = keep.tile([P, N], BF16, name="crow")
-        nc.gpsimd.memset(crow[:], 0.0)
-        ones = keep.tile([P, P], BF16, name="ones")
-        nc.gpsimd.memset(ones[:], 1.0)
-        cb = keep.tile([P, N], F32, name="cb")
+        cb = keep.tile([P, N], BF16, name="cb")
 
         def load_x(lo, hi):
             nc.sync.dma_start(
@@ -78,7 +74,8 @@ def tile_maxout_then_linear_f7_kernel(tc, x_bytes, x_scale, w_words, w_scales, b
                 )
 
         load_x(0, 1)
-        load_x(1, 4)
+        load_x(1, 2)
+        load_x(2, 4)
         load_scales(ws, w_scales)
         load_w(0)
         nc.sync.dma_start(out=braw[0:24, :], in_=b.rearrange("j (t p) -> (j t) p", p=P))
@@ -90,7 +87,7 @@ def tile_maxout_then_linear_f7_kernel(tc, x_bytes, x_scale, w_words, w_scales, b
         for g in range(2):
             nc.sync.dma_start(out=vt[:, g].bitcast(I32), in_=v_words[g].rearrange("p n t -> p (n t)").bitcast(I32))
         load_scales(vs, v_scales)
-        nc.sync.dma_start(out=crow[0:1, :], in_=c.unsqueeze(0))
+        nc.sync.dma_start(out=cb[:], in_=c.partition_broadcast(P))
 
         xc = [keep.tile([P, 2, ROWS], U32, name="xc%d" % i, align_bytes=64) for i in range(HALVES)]
         xcs = [keep.tile([P, 2, ROWS], U8, name="xcs%d" % i, align_bytes=64) for i in range(HALVES)]
@@ -273,7 +270,7 @@ def tile_maxout_then_linear_f7_kernel(tc, x_bytes, x_scale, w_words, w_scales, b
         x_cast(2, "s")
         x_both(x_out, 0)
         x_turn(1)
-        keep_warm(1)
+        keep_warm(2)
         x_both(x_quant, 0)
         x_both(x_out, 1)
         x_cast(3, "s")
@@ -291,13 +288,13 @@ def tile_maxout_then_linear_f7_kernel(tc, x_bytes, x_scale, w_words, w_scales, b
         nc.tensor.transpose(bps, bf32[:], ident[:])
         x_out(3, 0)
         x_cast(5, "s")
+        x_cast(6, "s")
         nc.scalar.copy(out=bias[:], in_=bps[:, 0:24])
         x_both(x_quant, 2)
         x_out(3, 1)
         head_mul(2)
         x_both(x_quant, 3)
         head_mul(3)
-        x_cast(6, "s")
         x_both(x_out, 4)
         x_both(x_quant, 4)
 
@@ -324,33 +321,32 @@ def tile_maxout_then_linear_f7_kernel(tc, x_bytes, x_scale, w_words, w_scales, b
                 h_weave(1, 0, 0, "s")
             h_max(s)
             h_move(s)
-            for q in ready:
-                h_quant(*q)
+            if s < 15:
+                for q in ready:
+                    h_quant(*q)
             if 1 <= s <= 6:
                 x_quant(i, g)
-            if s == 8:
-                for n in range(2):
-                    cps = tpool.tile([P, 512], F32, name="xt")
-                    nc.tensor.matmul(cps[:], lhsT=ones[:], rhs=crow[:, n * 512 : (n + 1) * 512], start=True, stop=True)
-                    nc.scalar.copy(out=cb[:, n * 512 : (n + 1) * 512], in_=cps[:])
         def y_done(half, r, n, how):
             y_out(half, r, n, how)
             y_store(half, r, n * 512, (n + 1) * 512)
 
-        for q in pend:
-            h_quant(*q)
-        for r in range(4):
+        for r in (0, 1):
             y_mul(0, r, 0)
             y_mul(0, r, 1)
         y_done(0, 0, 0, "v")
         y_done(0, 0, 1, "s")
         h_weave(1, 0, 1, "s")
+        for r in (2, 3):
+            h_quant(0, 1, r)
+            y_mul(0, r, 0)
+            y_mul(0, r, 1)
+        h_quant(1, 0, 0)
         y_done(0, 1, 0, "v")
         y_done(0, 1, 1, "s")
         h_weave(1, 0, 2, "s")
         h_quant(1, 0, 1)
         y_done(0, 2, 0, "v")
-        y_done(0, 2, 1, "s")
+        y_done(0, 2, 1, "v")
         h_weave(1, 0, 3, "s")
         y_done(0, 3, 0, "v")
         h_weave(1, 1, 0, "v")

from contextlib import ExitStack

import concourse.mybir as mybir
from concourse.masks import make_identity

M, K, F, PIECES, N = 1024, 1024, 1024, 3, 1024
FLOPS = 2 * M * K * PIECES * F + 2 * M * F * N

F32 = mybir.dt.float32
BF16 = mybir.dt.bfloat16
I32 = mybir.dt.int32
U32 = mybir.dt.uint32
U8 = mybir.dt.uint8
E4M3 = mybir.dt.float8_e4m3fn
FP8X4 = mybir.dt.float8_e4m3fn_x4
FP4X4 = mybir.dt.float4_e2m1fn_x4
ALU = mybir.AluOpType
ACT = mybir.ActivationFunctionType

P = 128
ROWS = 512
HALVES = M // ROWS
TILES = F // P


def tile_maxout_then_linear_f7_kernel(tc, x_bytes, x_scale, w_words, w_scales, b, v_words, v_scales, c, out):
    nc = tc.nc
    with ExitStack() as ctx:
        keep = ctx.enter_context(tc.tile_pool(name="keep", bufs=1))
        stage = ctx.enter_context(tc.tile_pool(name="stage", bufs=4))
        deep = ctx.enter_context(tc.tile_pool(name="deep", bufs=8))
        zpool = ctx.enter_context(tc.psum_pool(name="zpool", bufs=6))
        tpool = ctx.enter_context(tc.psum_pool(name="tpool", bufs=2))
        ctx.enter_context(tc.manual_schedule())

        sc = keep.tile([P, 2, 2, 2], F32, name="sc")
        nc.scalar.dma_start(
            out=sc[:].rearrange("p g u e -> p g (u e)"), in_=x_scale.rearrange("o (g p t) -> p (o g) t", g=2, t=4)
        )
        ident = keep.tile([P, P], F32, name="ident")
        make_identity(nc, ident[:])
        braw = keep.tile([P, P], BF16, name="braw")
        warm = keep.tile([P, 512], BF16, name="warm")
        nc.vector.memset(warm[:], 0.0)
        nc.gpsimd.memset(braw[:], 0.0)
        ws = keep.tile([P, 2, PIECES * F], U8, name="ws", align_bytes=64)
        nc.vector.memset(ws[:].rearrange("p g n -> p (g n)").bitcast(U32), 0)
        vs = keep.tile([P, 2, N], U8, name="vs", align_bytes=64)
        nc.gpsimd.memset(vs[:].rearrange("p g n -> p (g n)").bitcast(U32), 0)

        xb4 = [keep.tile([P, 4, K], U8, name="xb%d" % i, align_bytes=64) for i in range(2)]
        xb = [xb4[i // 4][:, i % 4] for i in range(8)]
        wt = [keep.tile([P, 2, PIECES, 512], U8, name="wt%d" % q, align_bytes=64) for q in range(4)]
        vt = keep.tile([P, 2, 4 * N], U8, name="vt", align_bytes=64)
        cb = keep.tile([P, N], BF16, name="cb")

        def load_x(lo, hi):
            nc.sync.dma_start(
                out=xb4[lo // 4][:, lo % 4 : lo % 4 + hi - lo], in_=x_bytes[lo * P : hi * P, :].rearrange("(r p) k -> p r k", p=P)
            )

        def load_w(q):
            for g in range(2):
                nc.sync.dma_start(
                    out=wt[q][:, g].bitcast(I32),
                    in_=w_words[g].rearrange("p (j n) -> p j n", j=PIECES)[:, :, q * 512 : (q + 1) * 512].bitcast(I32),
                )

        def load_scales(tile, scales):
            for q in range(4):
                nc.sync.dma_start(
                    out=tile[32 * q : 32 * q + 4].bitcast(I32),
                    in_=scales[:, 4 * q : 4 * q + 4, :].rearrange("g q n -> q g n").bitcast(I32),
                )

        load_x(0, 1)
        load_x(1, 2)
        load_x(2, 4)
        load_scales(ws, w_scales)
        load_w(0)
        nc.sync.dma_start(out=braw[0:24, :], in_=b.rearrange("j (t p) -> (j t) p", p=P))
        load_x(4, 6)
        load_w(1)
        load_x(6, 8)
        load_w(2)
        load_w(3)
        for g in range(2):
            nc.sync.dma_start(out=vt[:, g].bitcast(I32), in_=v_words[g].rearrange("p n t -> p (n t)").bitcast(I32))
        load_scales(vs, v_scales)
        nc.sync.dma_start(out=cb[:], in_=c.partition_broadcast(P))

        xc = [keep.tile([P, 2, ROWS], U32, name="xc%d" % i, align_bytes=64) for i in range(HALVES)]
        xcs = [keep.tile([P, 2, ROWS], U8, name="xcs%d" % i, align_bytes=64) for i in range(HALVES)]
        hc = [keep.tile([P, 2, ROWS], U32, name="hc%d" % i, align_bytes=64) for i in range(HALVES)]
        hcs = [keep.tile([P, 2, ROWS], U8, name="hcs%d" % i, align_bytes=64) for i in range(HALVES)]
        hp = [[keep.tile([P, 4, ROWS], BF16, name="hp%d%d" % (i, g), align_bytes=64) for g in range(2)] for i in range(HALVES)]
        bias = keep.tile([P, 24], F32, name="bias")
        bf32 = keep.tile([P, P], F32, name="bf32")

        xw, xt, xg = {}, {}, {}

        def x_cast(i, engine):
            w = deep.tile([P, K], BF16, name="xw", align_bytes=64)
            if engine == "v":
                for g in range(2):
                    nc.vector.tensor_copy(out=w[:, g * 512 : (g + 1) * 512], in_=xb[i][:, g * 512 : (g + 1) * 512].bitcast(E4M3))
            else:
                nc.scalar.copy(out=w[:], in_=xb[i].bitcast(E4M3))
            xw[i] = w

        def x_turn(i):
            words = xw[i][:].bitcast(F32)
            t = tpool.tile([P, 2, 2, P], F32, name="xt")
            for g in range(2):
                for u in range(2):
                    nc.tensor.transpose(t[:, g, u, :], words[:, 256 * g + u : 256 * (g + 1) : 2], ident[:])
            xt[i] = t

        def x_out(i, g):
            if g == 0:
                a = stage.tile([P, 2, P, 4], BF16, name="xg", align_bytes=64)
                xg[i] = a
            a = xg[i]
            if True:
                nc.vector.tensor_tensor(
                    out=a[:, g].rearrange("p m (u e) -> p m u e", u=2),
                    in0=xt[i][:, g].bitcast(BF16).rearrange("p u (m e) -> p m u e", e=2),
                    in1=sc[:, g].unsqueeze(1).to_broadcast([P, P, 2, 2]),
                    op=ALU.mult,
                )

        def x_quant(i, g):
            half, r = i // 4, i % 4
            if True:
                nc.vector.quantize_mx(
                    out=xc[half][:, g, r * P : (r + 1) * P].bitcast(FP8X4),
                    scales=xcs[half][:, g, r * P : (r + 1) * P],
                    in_=xg[i][:, g].rearrange("p m t -> p (m t)"),
                )

        zs, us, vv, hh = {}, {}, {}, {}

        def z_new(s):
            zs[s] = []
            for j in range(PIECES):
                z = zpool.tile([P, ROWS], F32, name="z")
                zs[s].append(z)

        def z_mul(s, lo, hi):
            half, T = s // TILES, s % TILES
            col = (T % 2) * 256
            for j in range(PIECES):
                for g in range(2):
                    nc.tensor.matmul_mx(
                        out=zs[s][j][:, lo:hi],
                        lhsT=wt[T // 2][:, g, j, col : col + 256].bitcast(FP4X4),
                        lhsT_scale=ws[:, g, j * F + T * P : j * F + (T + 1) * P],
                        rhs=xc[half][:, g, lo:hi].bitcast(FP8X4),
                        rhs_scale=xcs[half][:, g, lo:hi],
                        start=(g == 0),
                        stop=(g == 1),
                    )

        def u_out(s, pieces=2):
            T = s % TILES
            us[s] = []
            for j in range(pieces):
                u = stage.tile([P, ROWS], BF16, name="u%d" % j, align_bytes=64)
                nc.scalar.activation(out=u[:], in_=zs[s][j][:], func=ACT.Identity, bias=bias[:, 8 * j + T : 8 * j + T + 1])
                us[s].append(u)

        def v_max(s):
            v = stage.tile([P, ROWS], BF16, name="v", align_bytes=64)
            nc.vector.tensor_tensor(out=v[:], in0=us[s][0][:], in1=us[s][1][:], op=ALU.max)
            vv[s] = v

        def h_max(s):
            T = s % TILES
            h = stage.tile([P, ROWS], BF16, name="h", align_bytes=64)
            hh[s] = h
            if len(us[s]) == 3:
                nc.vector.tensor_tensor(out=h[:], in0=us[s][2][:], in1=vv[s][:], op=ALU.max)
                return
            nc.vector.scalar_tensor_tensor(
                out=h[:], in0=zs[s][2][:], scalar=bias[:, 16 + T : 17 + T], in1=vv[s][:], op0=ALU.add, op1=ALU.max
            )

        def h_move(s):
            half, T = s // TILES, s % TILES
            g, q = T // 4, T % 4
            for t in range(4):
                nc.sync.dma_start(out=hp[half][g][32 * q : 32 * q + 32, t, :], in_=hh[s][t:P:4, :])

        hg = {}

        def h_weave(half, g, r, engine):
            a = deep.tile([P, P, 4], BF16, name="hg", align_bytes=64)
            src = hp[half][g][:, :, r * P : (r + 1) * P].rearrange("p t m -> p m t")
            if engine == "v":
                nc.vector.tensor_copy(out=a[:], in_=src)
            else:
                nc.scalar.copy(out=a[:], in_=src)
            hg[(half, g, r)] = a

        def h_quant(half, g, r):
            nc.vector.quantize_mx(
                out=hc[half][:, g, r * P : (r + 1) * P].bitcast(FP8X4),
                scales=hcs[half][:, g, r * P : (r + 1) * P],
                in_=hg[(half, g, r)][:].rearrange("p m t -> p (m t)"),
            )

        ys, yt = {}, {}

        def y_mul(half, r, g):
            for n in range(2):
                if g == 0:
                    if r == 3:
                        y = tpool.tile([P, ROWS], F32, name="xt")
                    else:
                        y = zpool.tile([P, ROWS], F32, name="z")
                    ys[(half, r, n)] = y
                nc.tensor.matmul_mx(
                    out=ys[(half, r, n)][:],
                    lhsT=hc[half][:, g, r * P : (r + 1) * P].bitcast(FP8X4),
                    lhsT_scale=hcs[half][:, g, r * P : (r + 1) * P],
                    rhs=vt[:, g, n * 2048 : (n + 1) * 2048].bitcast(FP8X4),
                    rhs_scale=vs[:, g, n * 512 : (n + 1) * 512],
                    start=(g == 0),
                    stop=(g == 1),
                )

        def y_out(half, r, n, how):
            if n == 0:
                o = deep.tile([P, N], F32, name="yt")
                yt[(half, r)] = o
            o = yt[(half, r)]
            cols = slice(n * 512, (n + 1) * 512)
            y = ys[(half, r, n)]
            if how == "v":
                nc.vector.tensor_tensor(out=o[:, cols], in0=y[:], in1=cb[:, cols], op=ALU.add)
            else:
                e = stage.tile([P, 512], F32, name="ye")
                nc.scalar.copy(out=e[:], in_=y[:])
                nc.gpsimd.tensor_tensor(out=o[:, cols], in0=e[:], in1=cb[:, cols], op=ALU.add)

        def y_store(half, r, lo=0, hi=N):
            m0 = half * ROWS + r * P
            nc.sync.dma_start(out=out[m0 : m0 + P, lo:hi], in_=yt[(half, r)][:, lo:hi])

        z_new(0)
        z_new(1)

        def head_mul(r):
            z_mul(0, r * P, (r + 1) * P)
            z_mul(1, r * P, (r + 1) * P)

        def x_both(f, i):
            f(i, 0)
            f(i, 1)

        def keep_warm(times):
            for i in range(times):
                nc.tensor.matmul(zs[1][2][:], lhsT=warm[:, 0:P], rhs=warm[:], start=True, stop=True)

        keep_warm(5)
        x_cast(0, "v")
        x_cast(1, "s")
        x_turn(0)
        keep_warm(2)
        x_cast(2, "s")
        x_both(x_out, 0)
        x_turn(1)
        keep_warm(2)
        x_both(x_quant, 0)
        x_both(x_out, 1)
        x_cast(3, "s")
        x_turn(2)
        head_mul(0)
        x_out(2, 0)
        x_both(x_quant, 1)
        x_out(2, 1)
        nc.scalar.copy(out=bf32[:], in_=braw[:])
        x_cast(4, "s")
        x_turn(3)
        head_mul(1)
        x_turn(4)
        bps = zs[1][2][:, 3 * P : 4 * P]
        nc.tensor.transpose(bps, bf32[:], ident[:])
        x_out(3, 0)
        x_cast(5, "s")
        x_cast(6, "s")
        nc.scalar.copy(out=bias[:], in_=bps[:, 0:24])
        x_both(x_quant, 2)
        x_out(3, 1)
        head_mul(2)
        x_both(x_quant, 3)
        head_mul(3)
        x_both(x_out, 4)
        x_both(x_quant, 4)

        pend = []
        for s in range(16):
            if s >= 2:
                z_new(s)
                z_mul(s, 0, ROWS)
            u_out(s, 3 if s == 15 else 2)
            if s == 1:
                x_cast(7, "s")
            ready, pend = pend, []
            if s in (0, 1, 4):
                x_turn((5, 6, 0, 0, 7)[s])
            v_max(s)
            if 1 <= s <= 6:
                i, g = 5 + (s - 1) // 2, (s - 1) % 2
                x_out(i, g)
            if 8 <= s:
                pend.append((0, (s - 8) // 4, s % 4))
                h_weave(*pend[-1], "v")
            if s == 14:
                pend.append((1, 0, 0))
                h_weave(1, 0, 0, "s")
            h_max(s)
            h_move(s)
            if s < 15:
                for q in ready:
                    h_quant(*q)
            if 1 <= s <= 6:
                x_quant(i, g)
        def y_done(half, r, n, how):
            y_out(half, r, n, how)
            y_store(half, r, n * 512, (n + 1) * 512)

        for r in (0, 1):
            y_mul(0, r, 0)
            y_mul(0, r, 1)
        y_done(0, 0, 0, "v")
        y_done(0, 0, 1, "s")
        h_weave(1, 0, 1, "s")
        for r in (2, 3):
            h_quant(0, 1, r)
            y_mul(0, r, 0)
            y_mul(0, r, 1)
        h_quant(1, 0, 0)
        y_done(0, 1, 0, "v")
        y_done(0, 1, 1, "s")
        h_weave(1, 0, 2, "s")
        h_quant(1, 0, 1)
        y_done(0, 2, 0, "v")
        y_done(0, 2, 1, "v")
        h_weave(1, 0, 3, "s")
        y_done(0, 3, 0, "v")
        h_weave(1, 1, 0, "v")
        h_weave(1, 1, 1, "s")
        h_quant(1, 0, 2)
        h_quant(1, 1, 0)
        h_weave(1, 1, 2, "s")
        y_done(0, 3, 1, "v")
        h_weave(1, 1, 3, "s")
        for r in range(3):
            y_mul(1, r, 0)
        h_quant(1, 1, 1)
        h_quant(1, 0, 3)
        y_mul(1, 0, 1)
        y_mul(1, 1, 1)
        y_mul(1, 3, 0)
        y_out(1, 0, 0, "v")
        h_quant(1, 1, 2)
        y_mul(1, 2, 1)
        y_out(1, 0, 1, "s")
        h_quant(1, 1, 3)
        y_mul(1, 3, 1)
        for r, n, how in ((1, 0, "v"), (1, 1, "s"), (2, 0, "v"), (2, 1, "v"), (3, 0, "v"), (3, 1, "v")):
            y_out(1, r, n, how)
        for r, n in ((0, 0), (1, 0), (0, 1), (2, 0), (2, 1), (1, 1), (3, 0), (3, 1)):
            y_store(1, r, n * 512, (n + 1) * 512)
